import numpy as np, ml_dtypes
CORES = [0,8,16,24,32,40,48,56,64,72,80,88,96,104,112,120]
N = 16
T = 8
ROUTE = [[[9,15,6,5],[13,11,10,5],[12,13,2,14],[5,8,7,11],[9,13,4,7],[6,11,12,14],[15,0,8,6],[9,2,15,7]],[[7,12,11,5],[13,8,14,5],[1,10,9,14],[9,15,2,8],[13,10,4,3],[15,12,0,2],[10,8,4,15],[6,13,0,15]],[[5,3,15,7],[9,1,14,12],[10,0,6,2],[7,2,8,5],[15,11,8,6],[1,0,13,8],[12,11,10,3],[15,2,5,14]],[[13,10,7,12],[8,13,9,7],[2,1,6,15],[2,12,7,10],[8,12,7,4],[9,10,1,7],[15,3,11,0],[13,7,1,6]],[[3,12,7,15],[6,7,12,3],[1,3,5,10],[6,10,7,2],[12,3,4,2],[7,3,12,11],[8,7,4,2],[11,1,6,8]],[[6,4,11,12],[14,7,6,1],[12,7,10,0],[10,15,7,8],[12,15,5,6],[9,5,2,13],[6,7,1,8],[6,7,9,14]],[[0,11,6,5],[10,4,3,8],[11,14,3,7],[5,2,11,12],[12,8,3,0],[7,5,12,10],[7,6,11,4],[2,9,11,1]],[[6,12,3,1],[6,13,3,9],[9,4,15,2],[5,3,7,10],[0,1,12,3],[9,5,15,8],[3,8,6,7],[13,11,0,5]],[[6,1,7,15],[9,14,8,15],[9,2,0,14],[8,15,1,4],[10,3,4,2],[4,7,10,5],[11,5,7,6],[6,9,11,13]],[[1,15,0,11],[8,6,10,14],[11,15,7,13],[8,3,9,6],[9,0,5,15],[5,4,0,12],[1,10,7,13],[2,1,11,12]],[[7,3,14,10],[5,9,4,13],[7,6,10,4],[3,5,15,4],[10,1,9,14],[12,15,5,9],[4,2,14,10],[14,11,4,15]],[[6,10,9,3],[4,11,9,5],[0,15,13,7],[1,15,9,6],[1,15,11,13],[13,14,2,15],[9,14,6,4],[1,0,12,11]],[[4,9,6,3],[8,4,0,5],[1,6,9,13],[3,1,14,4],[8,4,14,11],[9,1,0,2],[9,7,12,8],[1,5,3,13]],[[0,6,7,4],[3,8,9,12],[0,12,10,13],[10,9,15,6],[14,8,11,15],[11,15,10,5],[15,13,3,6],[7,6,11,0]],[[15,6,14,10],[6,9,10,12],[2,11,14,15],[2,0,14,10],[14,12,10,13],[12,2,11,0],[10,9,8,2],[9,13,2,11]],[[8,1,10,2],[1,4,9,6],[9,12,1,5],[12,2,15,11],[4,10,11,8],[2,1,13,11],[5,12,13,7],[7,8,10,5]]]
YW = 40
def setup_inputs(rng):
    return {"x": rng.standard_normal((N, 128, T), dtype=np.float32).astype(ml_dtypes.bfloat16)}
def reference(x):
    y = np.full((N, 128, YW), np.nan, x.dtype)
    fill = [0] * N
    for r in range(N):
        for t in range(T):
            for e in ROUTE[r][t]:
                y[e][:, fill[e]] = x[r][:, t]
                fill[e] += 1
    return {"y": y}

@@ -1,0 +1,204 @@
+from concourse.bass import DstId, RemoteDMATransfer
+
+SCRATCH = {
+    "xs": ("sbuf", [128, 8], "bfloat16"),
+    "ybuf": ("sbuf", [128, 40], "bfloat16"),
+}
+SEMAPHORES = ["loaded", "got", "sent", "arrived", "stored"]
+
+CROSS = (2, 3, 6, 7)
+PLAIN = (0, 1, 4, 5)
+CACHE = {}
+
+
+def chunks(items, n):
+    return [items[i:i + n] for i in range(0, len(items), n)]
+
+
+def pieces(route, r, nranks, off, split):
+    cls = ([], [], [])
+    left = list(split)
+    for e in range(nranks):
+        ts = [t for t in range(len(route[r])) if e in route[r][t]]
+        k = 2 if e == r else (0 if (e ^ r) & 1 else 1)
+        i = 0
+        while i < len(ts):
+            if i + 1 < len(ts) and ts[i + 1] == ts[i] + 1 and (k == 2 or left[k] == 0):
+                cls[k].append((ts[i], 2, e, off[(r, ts[i], e)]))
+                i += 2
+            else:
+                if i + 1 < len(ts) and ts[i + 1] == ts[i] + 1:
+                    left[k] -= 1
+                    cls[k].append((ts[i], 1, e, off[(r, ts[i], e)]))
+                    i += 1
+                cls[k].append((ts[i], 1, e, off[(r, ts[i], e)]))
+                i += 1
+    return cls
+
+
+def pack(items, cores, bins):
+    by_w = {1: sorted(x for x in items if x[1] == 1), 2: sorted(x for x in items if x[1] == 2)}
+    for c in cores:
+        b = bins.get(c)
+        if b and len({x[1] for x in b}) == 1:
+            w = b[0][1]
+            while len(b) < 4 and by_w[w]:
+                b.append(by_w[w].pop(0))
+    free = [c for c in cores if not bins.get(c)]
+    parts = chunks(by_w[2], 4) + chunks(by_w[1], 4)
+    if len(parts) > len(free):
+        a, b = chunks(by_w[2], 4), chunks(by_w[1], 4)
+        if a and b and len(a[-1]) + len(b[-1]) <= 4:
+            parts = a[:-1] + b[:-1] + [a[-1] + b[-1]]
+    if len(parts) > len(free):
+        return False
+    parts.sort(key=lambda p: (-len({x[1] for x in p}), -len(p)))
+    for c, p in zip(free, parts):
+        bins[c] = list(p)
+    return True
+
+
+def plan_rank(route, r, nranks, off):
+    best = None
+    for s0 in range(0, 7):
+        for s1 in range(0, 7):
+            cross, same, own = pieces(route, r, nranks, off, (s0, s1))
+            bins = {}
+            if not pack(cross, CROSS, bins):
+                continue
+            if not pack(same, (0,) + CROSS + PLAIN[1:], bins):
+                continue
+            two = sum(1 for b in bins.values() if len({x[1] for x in b}) > 1)
+            cost = (two, len([c for c in bins if c != 0]), len(cross) + len(same))
+            if best is None or cost < best[0]:
+                best = (cost, bins, own)
+    return best[1], best[2]
+
+
+def engines(groups, base):
+    n = len(groups)
+    best = None
+    stack = [[]]
+    while stack:
+        m = stack.pop()
+        if len(m) == n:
+            if sum(m) <= 8:
+                cost = (max(len(gr) / k for gr, k in zip(groups, m)), sum(len(gr) / k for gr, k in zip(groups, m)))
+                if best is None or cost < best[0]:
+                    best = (cost, m)
+            continue
+        for k in (1, 2, 4, 8):
+            if sum(m) + k <= 8:
+                stack.append(m + [k])
+    out, bit = [], base
+    for k in best[1]:
+        out.append((((1 << k) - 1) << bit, k))
+        bit += k
+    return best[0][0], out
+
+
+def group(writes):
+    keys = sorted({(x[1], x[0]) for x in writes}, reverse=True)
+    whole = [[x for x in writes if (x[1], x[0]) == k] for k in keys]
+    cut = [p for gr in whole for p in chunks(gr, 2)]
+    single = [[x] for gr in whole for x in gr]
+    best = None
+    for cand in (whole, cut, single):
+        if len(cand) > 8:
+            continue
+        c, masks = engines(cand, 0)
+        if best is None or c < best[0]:
+            best = (c, cand)
+    return best[1]
+
+
+def make_plan(route, nranks):
+    off, fill = {}, [0] * nranks
+    for r in range(nranks):
+        for t in range(len(route[r])):
+            for e in route[r][t]:
+                off[(r, t, e)] = fill[e]
+                fill[e] += 1
+    plan, need = [], [0] * nranks
+    for r in range(nranks):
+        bins, own = plan_rank(route, r, nranks, off)
+        helpers = sorted((c for c in bins if c != 0),
+                         key=lambda c: (-len({x[1] for x in bins[c]}), -len(bins[c]), c not in CROSS, c))
+        home = {c: [] for c in helpers}
+        todo = []
+        for (t, w, e, col) in own:
+            if w == 2 and not any(x[1] == 2 for c in helpers for x in bins[c]):
+                todo += [(t, 1, e, col), (t + 1, 1, e, col + 1)]
+            else:
+                todo.append((t, w, e, col))
+        for x in todo:
+            fit = [c for c in helpers if any(y[1] == x[1] for y in bins[c])] or helpers
+            c = min(fit, key=lambda c: (len(home[c]), helpers.index(c)))
+            home[c].append(x)
+        calls = {}
+        for c in bins:
+            trs = []
+            gs = group(bins[c])
+            for gr, (mask, k) in zip(gs, engines(gs, 0)[1]):
+                trs.append((gr[0][0], gr[0][1], mask, k, [(x[2], x[3]) for x in gr]))
+            hs = [[x] for x in home.get(c, [])]
+            if hs:
+                for gr, (mask, k) in zip(hs, engines(hs, 8)[1]):
+                    trs.append((gr[0][0], gr[0][1], mask, k, [(x[2], x[3]) for x in gr]))
+            widths = sorted({tr[1] for tr in trs}, key=lambda w: -max(len(tr[4]) / tr[3] for tr in trs if tr[1] == w))
+            calls[c] = [[tr for tr in trs if tr[1] == w] for w in widths]
+            for tr in trs:
+                for (e, col) in tr[4]:
+                    need[e] += tr[3]
+        plan.append((helpers, calls))
+    return plan, need, fill
+
+
+def rank_program(g, core, T, topo):
+    route = T.tables["ROUTE"]
+    nranks = len(T.cores)
+    if "plan" not in CACHE:
+        CACHE["plan"] = make_plan(route, nranks)
+    plan, need, fill = CACHE["plan"]
+    base = core - core % 8
+    rank = T.rank_of(base)
+    if rank is None:
+        return
+    helpers, calls = plan[rank]
+    k = core % 8
+    if k != 0 and k not in helpers:
+        return
+    sem = T.sem
+
+    def dst(c):
+        rid, pid, _se = topo.addr(c)
+        return DstId(rid=rid, pnc=pid)
+
+    def scatter():
+        total = 0
+        for call in calls.get(k, []):
+            trs = []
+            for (t, w, mask, n, dsts) in call:
+                trs.append(RemoteDMATransfer(
+                    dst_ids=[dst(T.cores[e]) for (e, col) in dsts], dma_engine_mask=mask, remote_sem=sem.arrived,
+                    srcs=[T.xs[:, t:t + w]], dsts=[T.ybuf[:, col:col + w] for (e, col) in dsts]))
+                total += n
+            g.remote_dma_fused(trs, local_sem=sem.sent)
+        return total
+
+    if k != 0:
+        g.wait_ge(sem.got, 16)
+        g.wait_ge(sem.sent, scatter())
+        return
+
+    g.sync.dma_start(T.xs[:], T.x[:]).then_inc(sem.loaded, 16)
+    g.wait_ge(sem.loaded, 16)
+    g.remote_dma_fused([RemoteDMATransfer(
+        dst_ids=[dst(base + h) for h in helpers], dma_engine_mask=0xFFFF, remote_sem=sem.got,
+        srcs=[T.xs[:]], dsts=[T.xs[:] for h in helpers])], local_sem=sem.sent)
+    total = 16 + scatter()
+    n = fill[rank]
+    g.sync.wait_ge(sem.arrived, need[rank])
+    g.sync.dma_start(T.y[:, 0:n], T.ybuf[:, 0:n]).then_inc(sem.stored, 16)
+    g.wait_ge(sem.sent, total)
+    g.wait_ge(sem.stored, 16)

@@ -1,13 +1,13 @@
 from concourse.bass import DstId, RemoteDMATransfer
 
 SCRATCH = {
+    "xd": ("dram", [128, 8], "bfloat16"),
     "xs": ("sbuf", [128, 8], "bfloat16"),
     "ybuf": ("sbuf", [128, 40], "bfloat16"),
 }
-SEMAPHORES = ["loaded", "got", "sent", "arrived", "stored"]
+SEMAPHORES = ["copied", "loaded", "got", "sent", "arrived", "stored"]
 
 CROSS = (2, 3, 6, 7)
-PLAIN = (0, 1, 4, 5)
 CACHE = {}
 
 
@@ -36,43 +36,68 @@ def pieces(route, r, nranks, off, split):
     return cls
 
 
-def pack(items, cores, bins):
-    by_w = {1: sorted(x for x in items if x[1] == 1), 2: sorted(x for x in items if x[1] == 2)}
-    for c in cores:
-        b = bins.get(c)
-        if b and len({x[1] for x in b}) == 1:
-            w = b[0][1]
-            while len(b) < 4 and by_w[w]:
-                b.append(by_w[w].pop(0))
-    free = [c for c in cores if not bins.get(c)]
-    parts = chunks(by_w[2], 4) + chunks(by_w[1], 4)
-    if len(parts) > len(free):
-        a, b = chunks(by_w[2], 4), chunks(by_w[1], 4)
-        if a and b and len(a[-1]) + len(b[-1]) <= 4:
-            parts = a[:-1] + b[:-1] + [a[-1] + b[-1]]
-    if len(parts) > len(free):
-        return False
-    parts.sort(key=lambda p: (-len({x[1] for x in p}), -len(p)))
-    for c, p in zip(free, parts):
-        bins[c] = list(p)
-    return True
+PATTERN = {0: (), 1: (1,), 2: (2,), 3: (2, 1), 4: (4,), 5: (4, 1), 6: (4, 2)}
+ORDER = (2, 3, 6, 7, 1, 4, 5)
+CREDIT = 16
 
 
-def plan_rank(route, r, nranks, off):
+def width_choices(slots):
+    out = {}
+    for bits in range(1 << len(slots)):
+        idx = [i for i in range(len(slots)) if bits >> i & 1]
+        cap = sum(slots[i][1] for i in idx)
+        if cap not in out or len(idx) < len(out[cap]):
+            out[cap] = idx
+    return out
+
+
+def fill_slots(slots, two, cross, same):
+    held = [[] for s in slots]
+    for w in (2, 1):
+        mine = [i for i in range(len(slots)) if (i in two) == (w == 2)]
+        first = sorted((i for i in mine if slots[i][0] in CROSS), key=lambda i: -slots[i][1])
+        todo = sorted(x for x in cross if x[1] == w)
+        for i in first:
+            while todo and len(held[i]) < slots[i][1]:
+                held[i].append(todo.pop(0))
+        if todo:
+            return None
+        todo = sorted(x for x in same if x[1] == w)
+        rest = sorted(mine, key=lambda i: (not held[i], -slots[i][1], slots[i][0] != 0))
+        for i in rest:
+            while todo and len(held[i]) < slots[i][1]:
+                held[i].append(todo.pop(0))
+        if todo:
+            return None
+    bins = {}
+    for s, hw in zip(slots, held):
+        if hw:
+            bins.setdefault(s[0], []).append(hw)
+    return bins
+
+
+def plan_rank(route, r, nranks, off, x):
+    caps = {c: max(0, min(6, (x - 8 * (j + 1)) // 16)) for j, c in enumerate(ORDER)}
+    caps[0] = max(0, min(6, (x + CREDIT - 8 * len(ORDER)) // 16))
+    slots = [(c, n) for c in (0,) + ORDER for n in PATTERN[caps[c]]]
+    sc = [i for i in range(len(slots)) if slots[i][0] in CROSS]
+    sp = [i for i in range(len(slots)) if slots[i][0] not in CROSS]
+    wc = width_choices([slots[i] for i in sc])
+    wp = width_choices([slots[i] for i in sp])
     best = None
     for s0 in range(0, 7):
         for s1 in range(0, 7):
             cross, same, own = pieces(route, r, nranks, off, (s0, s1))
-            bins = {}
-            if not pack(cross, CROSS, bins):
-                continue
-            if not pack(same, (0,) + CROSS + PLAIN[1:], bins):
-                continue
-            two = sum(1 for b in bins.values() if len({x[1] for x in b}) > 1)
-            cost = (two, len([c for c in bins if c != 0]), len(cross) + len(same))
-            if best is None or cost < best[0]:
-                best = (cost, bins, own)
-    return best[1], best[2]
+            for ia in wc.values():
+                for ib in wp.values():
+                    two = {sc[i] for i in ia} | {sp[i] for i in ib}
+                    bins = fill_slots(slots, two, cross, same)
+                    if bins is None:
+                        continue
+                    cost = (sum(len(b) for b in bins.values()), len(bins), len(cross) + len(same))
+                    if best is None or cost < best[0]:
+                        best = (cost, bins, own)
+    return best and (best[1], best[2])
 
 
 def engines(groups, base):
@@ -119,37 +144,46 @@ def make_plan(route, nranks):
             for e in route[r][t]:
                 off[(r, t, e)] = fill[e]
                 fill[e] += 1
+    x, found = 80, None
+    while found is None:
+        x += 8
+        found = []
+        for r in range(nranks):
+            p = plan_rank(route, r, nranks, off, x)
+            if p is None:
+                found = None
+                break
+            found.append(p)
     plan, need = [], [0] * nranks
     for r in range(nranks):
-        bins, own = plan_rank(route, r, nranks, off)
-        helpers = sorted((c for c in bins if c != 0),
-                         key=lambda c: (-len({x[1] for x in bins[c]}), -len(bins[c]), c not in CROSS, c))
-        home = {c: [] for c in helpers}
+        bins, own = found[r]
+        helpers = [c for c in ORDER if c in bins]
+        home = {(c, i): [] for c in helpers for i in range(len(bins[c]))}
         todo = []
         for (t, w, e, col) in own:
-            if w == 2 and not any(x[1] == 2 for c in helpers for x in bins[c]):
+            if w == 2 and not any(bins[c][i][0][1] == 2 for (c, i) in home):
                 todo += [(t, 1, e, col), (t + 1, 1, e, col + 1)]
             else:
                 todo.append((t, w, e, col))
-        for x in todo:
-            fit = [c for c in helpers if any(y[1] == x[1] for y in bins[c])] or helpers
-            c = min(fit, key=lambda c: (len(home[c]), helpers.index(c)))
-            home[c].append(x)
+        for wr in todo:
+            fit = [k for k in home if bins[k[0]][k[1]][0][1] == wr[1]]
+            k = min(fit, key=lambda k: (len(home[k]), k[1], helpers.index(k[0])))
+            home[k].append(wr)
         calls = {}
         for c in bins:
-            trs = []
-            gs = group(bins[c])
-            for gr, (mask, k) in zip(gs, engines(gs, 0)[1]):
-                trs.append((gr[0][0], gr[0][1], mask, k, [(x[2], x[3]) for x in gr]))
-            hs = [[x] for x in home.get(c, [])]
-            if hs:
-                for gr, (mask, k) in zip(hs, engines(hs, 8)[1]):
-                    trs.append((gr[0][0], gr[0][1], mask, k, [(x[2], x[3]) for x in gr]))
-            widths = sorted({tr[1] for tr in trs}, key=lambda w: -max(len(tr[4]) / tr[3] for tr in trs if tr[1] == w))
-            calls[c] = [[tr for tr in trs if tr[1] == w] for w in widths]
-            for tr in trs:
-                for (e, col) in tr[4]:
-                    need[e] += tr[3]
+            calls[c] = []
+            for i, slot in enumerate(bins[c]):
+                trs = []
+                gs = group(slot)
+                hs = [[wr] for wr in home.get((c, i), [])]
+                for grs, base in ((gs, 0), (hs, 8)):
+                    if grs:
+                        for gr, (mask, k) in zip(grs, engines(grs, base)[1]):
+                            trs.append((gr[0][0], gr[0][1], mask, k, [(wr[2], wr[3]) for wr in gr]))
+                calls[c].append(trs)
+                for tr in trs:
+                    for (e, col) in tr[4]:
+                        need[e] += tr[3]
         plan.append((helpers, calls))
     return plan, need, fill
 
@@ -191,11 +225,13 @@ def rank_program(g, core, T, topo):
         g.wait_ge(sem.sent, scatter())
         return
 
+    g.sync.dma_start(T.xd[:], T.x[:]).then_inc(sem.copied, 16)
     g.sync.dma_start(T.xs[:], T.x[:]).then_inc(sem.loaded, 16)
-    g.wait_ge(sem.loaded, 16)
+    g.wait_ge(sem.copied, 16)
     g.remote_dma_fused([RemoteDMATransfer(
         dst_ids=[dst(base + h) for h in helpers], dma_engine_mask=0xFFFF, remote_sem=sem.got,
-        srcs=[T.xs[:]], dsts=[T.xs[:] for h in helpers])], local_sem=sem.sent)
+        srcs=[T.xd[:]], dsts=[T.xs[:] for h in helpers])], local_sem=sem.sent)
+    g.wait_ge(sem.loaded, 16)
     total = 16 + scatter()
     n = fill[rank]
     g.sync.wait_ge(sem.arrived, need[rank])

from concourse.bass import DstId, RemoteDMATransfer

SCRATCH = {
    "xd": ("dram", [128, 8], "bfloat16"),
    "xs": ("sbuf", [128, 8], "bfloat16"),
    "ybuf": ("sbuf", [128, 40], "bfloat16"),
}
SEMAPHORES = ["copied", "loaded", "got", "sent", "arrived", "stored"]

CROSS = (2, 3, 6, 7)
CACHE = {}


def chunks(items, n):
    return [items[i:i + n] for i in range(0, len(items), n)]


def pieces(route, r, nranks, off, split):
    cls = ([], [], [])
    left = list(split)
    for e in range(nranks):
        ts = [t for t in range(len(route[r])) if e in route[r][t]]
        k = 2 if e == r else (0 if (e ^ r) & 1 else 1)
        i = 0
        while i < len(ts):
            if i + 1 < len(ts) and ts[i + 1] == ts[i] + 1 and (k == 2 or left[k] == 0):
                cls[k].append((ts[i], 2, e, off[(r, ts[i], e)]))
                i += 2
            else:
                if i + 1 < len(ts) and ts[i + 1] == ts[i] + 1:
                    left[k] -= 1
                    cls[k].append((ts[i], 1, e, off[(r, ts[i], e)]))
                    i += 1
                cls[k].append((ts[i], 1, e, off[(r, ts[i], e)]))
                i += 1
    return cls


PATTERN = {0: (), 1: (1,), 2: (2,), 3: (2, 1), 4: (4,), 5: (4, 1), 6: (4, 2)}
ORDER = (2, 3, 6, 7, 1, 4, 5)
CREDIT = 16


def width_choices(slots):
    out = {}
    for bits in range(1 << len(slots)):
        idx = [i for i in range(len(slots)) if bits >> i & 1]
        cap = sum(slots[i][1] for i in idx)
        if cap not in out or len(idx) < len(out[cap]):
            out[cap] = idx
    return out


def fill_slots(slots, two, cross, same):
    held = [[] for s in slots]
    for w in (2, 1):
        mine = [i for i in range(len(slots)) if (i in two) == (w == 2)]
        first = sorted((i for i in mine if slots[i][0] in CROSS), key=lambda i: -slots[i][1])
        todo = sorted(x for x in cross if x[1] == w)
        for i in first:
            while todo and len(held[i]) < slots[i][1]:
                held[i].append(todo.pop(0))
        if todo:
            return None
        todo = sorted(x for x in same if x[1] == w)
        rest = sorted(mine, key=lambda i: (not held[i], -slots[i][1], slots[i][0] != 0))
        for i in rest:
            while todo and len(held[i]) < slots[i][1]:
                held[i].append(todo.pop(0))
        if todo:
            return None
    bins = {}
    for s, hw in zip(slots, held):
        if hw:
            bins.setdefault(s[0], []).append(hw)
    return bins


def plan_rank(route, r, nranks, off, x):
    caps = {c: max(0, min(6, (x - 8 * (j + 1)) // 16)) for j, c in enumerate(ORDER)}
    caps[0] = max(0, min(6, (x + CREDIT - 8 * len(ORDER)) // 16))
    slots = [(c, n) for c in (0,) + ORDER for n in PATTERN[caps[c]]]
    sc = [i for i in range(len(slots)) if slots[i][0] in CROSS]
    sp = [i for i in range(len(slots)) if slots[i][0] not in CROSS]
    wc = width_choices([slots[i] for i in sc])
    wp = width_choices([slots[i] for i in sp])
    best = None
    for s0 in range(0, 7):
        for s1 in range(0, 7):
            cross, same, own = pieces(route, r, nranks, off, (s0, s1))
            for ia in wc.values():
                for ib in wp.values():
                    two = {sc[i] for i in ia} | {sp[i] for i in ib}
                    bins = fill_slots(slots, two, cross, same)
                    if bins is None:
                        continue
                    cost = (sum(len(b) for b in bins.values()), len(bins), len(cross) + len(same))
                    if best is None or cost < best[0]:
                        best = (cost, bins, own)
    return best and (best[1], best[2])


def engines(groups, base):
    n = len(groups)
    best = None
    stack = [[]]
    while stack:
        m = stack.pop()
        if len(m) == n:
            if sum(m) <= 8:
                cost = (max(len(gr) / k for gr, k in zip(groups, m)), sum(len(gr) / k for gr, k in zip(groups, m)))
                if best is None or cost < best[0]:
                    best = (cost, m)
            continue
        for k in (1, 2, 4, 8):
            if sum(m) + k <= 8:
                stack.append(m + [k])
    out, bit = [], base
    for k in best[1]:
        out.append((((1 << k) - 1) << bit, k))
        bit += k
    return best[0][0], out


def group(writes):
    keys = sorted({(x[1], x[0]) for x in writes}, reverse=True)
    whole = [[x for x in writes if (x[1], x[0]) == k] for k in keys]
    cut = [p for gr in whole for p in chunks(gr, 2)]
    single = [[x] for gr in whole for x in gr]
    best = None
    for cand in (whole, cut, single):
        if len(cand) > 8:
            continue
        c, masks = engines(cand, 0)
        if best is None or c < best[0]:
            best = (c, cand)
    return best[1]


def make_plan(route, nranks):
    off, fill = {}, [0] * nranks
    for r in range(nranks):
        for t in range(len(route[r])):
            for e in route[r][t]:
                off[(r, t, e)] = fill[e]
                fill[e] += 1
    x, found = 80, None
    while found is None:
        x += 8
        found = []
        for r in range(nranks):
            p = plan_rank(route, r, nranks, off, x)
            if p is None:
                found = None
                break
            found.append(p)
    plan, need = [], [0] * nranks
    for r in range(nranks):
        bins, own = found[r]
        helpers = [c for c in ORDER if c in bins]
        home = {(c, i): [] for c in helpers for i in range(len(bins[c]))}
        todo = []
        for (t, w, e, col) in own:
            if w == 2 and not any(bins[c][i][0][1] == 2 for (c, i) in home):
                todo += [(t, 1, e, col), (t + 1, 1, e, col + 1)]
            else:
                todo.append((t, w, e, col))
        for wr in todo:
            fit = [k for k in home if bins[k[0]][k[1]][0][1] == wr[1]]
            k = min(fit, key=lambda k: (len(home[k]), k[1], helpers.index(k[0])))
            home[k].append(wr)
        calls = {}
        for c in bins:
            calls[c] = []
            for i, slot in enumerate(bins[c]):
                trs = []
                gs = group(slot)
                hs = [[wr] for wr in home.get((c, i), [])]
                for grs, base in ((gs, 0), (hs, 8)):
                    if grs:
                        for gr, (mask, k) in zip(grs, engines(grs, base)[1]):
                            trs.append((gr[0][0], gr[0][1], mask, k, [(wr[2], wr[3]) for wr in gr]))
                calls[c].append(trs)
                for tr in trs:
                    for (e, col) in tr[4]:
                        need[e] += tr[3]
        plan.append((helpers, calls))
    return plan, need, fill


def rank_program(g, core, T, topo):
    route = T.tables["ROUTE"]
    nranks = len(T.cores)
    if "plan" not in CACHE:
        CACHE["plan"] = make_plan(route, nranks)
    plan, need, fill = CACHE["plan"]
    base = core - core % 8
    rank = T.rank_of(base)
    if rank is None:
        return
    helpers, calls = plan[rank]
    k = core % 8
    if k != 0 and k not in helpers:
        return
    sem = T.sem

    def dst(c):
        rid, pid, _se = topo.addr(c)
        return DstId(rid=rid, pnc=pid)

    def scatter():
        total = 0
        for call in calls.get(k, []):
            trs = []
            for (t, w, mask, n, dsts) in call:
                trs.append(RemoteDMATransfer(
                    dst_ids=[dst(T.cores[e]) for (e, col) in dsts], dma_engine_mask=mask, remote_sem=sem.arrived,
                    srcs=[T.xs[:, t:t + w]], dsts=[T.ybuf[:, col:col + w] for (e, col) in dsts]))
                total += n
            g.remote_dma_fused(trs, local_sem=sem.sent)
        return total

    if k != 0:
        g.wait_ge(sem.got, 16)
        g.wait_ge(sem.sent, scatter())
        return

    g.sync.dma_start(T.xd[:], T.x[:]).then_inc(sem.copied, 16)
    g.sync.dma_start(T.xs[:], T.x[:]).then_inc(sem.loaded, 16)
    g.wait_ge(sem.copied, 16)
    g.remote_dma_fused([RemoteDMATransfer(
        dst_ids=[dst(base + h) for h in helpers], dma_engine_mask=0xFFFF, remote_sem=sem.got,
        srcs=[T.xd[:]], dsts=[T.xs[:] for h in helpers])], local_sem=sem.sent)
    g.wait_ge(sem.loaded, 16)
    total = 16 + scatter()
    n = fill[rank]
    g.sync.wait_ge(sem.arrived, need[rank])
    g.sync.dma_start(T.y[:, 0:n], T.ybuf[:, 0:n]).then_inc(sem.stored, 16)
    g.wait_ge(sem.sent, total)
    g.wait_ge(sem.stored, 16)
